import numpy as np
import ml_dtypes


def mxq(x, axis, fmt="e4m3"):
    dtype, down = {"e4m3": (ml_dtypes.float8_e4m3fn, 7), "e5m2": (ml_dtypes.float8_e5m2, 14)}[fmt]
    v = np.moveaxis(np.asarray(x, np.float32).astype(ml_dtypes.bfloat16).astype(np.float64), axis, -1)
    blocks = v.reshape(v.shape[:-1] + (-1, 32))
    amax = np.abs(blocks).max(-1, keepdims=True)
    byte = np.maximum(np.where(amax > 0, np.frexp(amax)[1] - 1 + 127, 0) - down, 1)
    scale = np.exp2(byte - 127.0)
    codes = (blocks / scale).astype(np.float32).astype(dtype).astype(np.float64)
    return np.moveaxis((codes * scale).reshape(v.shape), -1, axis)


WIDE = False


def mx_kscale(k):
    if not WIDE:
        return np.ones(k)
    levels = np.array([10, -10, 5, -5, 0])
    if k % 512:
        return np.exp2(np.random.permutation(np.resize(levels, k // 32))).repeat(32)
    a = np.empty((k // 512, 16))
    for p in range(k // 512):
        a[p, :8] = np.random.permutation(np.resize(levels, 8))
        for g in range(8):
            far = levels[np.abs(levels - a[p, g]) >= 10]
            a[p, g + 8] = far[np.random.randint(len(far))]
    return np.exp2(a.ravel()).repeat(32)


BF16 = ml_dtypes.bfloat16


def bf(x):
    return np.asarray(x, np.float32).astype(BF16)


def f64(x):
    return np.asarray(x).astype(np.float64)

def planes(Y):
    n, m = Y.shape
    b = f64(bf(Y)).reshape(n // 32, 32, m)
    amax = np.abs(b).max(1)
    byte = np.clip(np.where(amax > 0, np.frexp(amax)[1] - 1 + 127 - 7, 1), 1, 254)
    codes = (b * np.exp2(127.0 - byte)[:, None, :]).reshape(n, m).astype(np.float32).astype(ml_dtypes.float8_e4m3fn).view(np.uint8)
    words = codes.reshape(n // 512, 128, 4, m).transpose(0, 1, 3, 2)
    return np.ascontiguousarray(words), np.ascontiguousarray(byte.astype(np.uint8).reshape(n // 512, 16, m))


T, N, M = 1024, 1024, 1024


def soft_signed_links(t):
    return np.tanh(t) * (1.0 / (1.0 + np.exp(-4.0 * (np.abs(t) - 1.0))))


def setup_inputs():
    s, u = mx_kscale(T), mx_kscale(M)
    return {"x": bf(np.random.standard_normal((T, N)) * s[:, None]),
            "y": bf(np.random.standard_normal((T, M)) / s[:, None]),
            "w": bf((1.0 + 0.1 * np.random.standard_normal(M)) * u),
            "k": bf(np.random.standard_normal((M, M)) * (2.0 / np.sqrt(M)) / u[:, None])}


def core(x, y, w, k):
    steps = x.shape[0]
    t = (mxq(f64(x), 0, "e4m3").T @ mxq(f64(y), 0, "e4m3")) / np.sqrt(steps)
    a = soft_signed_links(t)
    aw = a * f64(w)[None, :]
    path = mxq(aw, 1, "e4m3") @ mxq(f64(k), 0, "e4m3")
    return path * a


def reference(x, y, w, k):
    R_out = core(x, y, w, k)
    words, scales = planes(R_out.T)
    return R_out, words, scales

from contextlib import ExitStack

import concourse.mybir as mybir
from concourse.masks import make_identity

T, N, M = 1024, 1024, 1024
FLOPS = 2 * T * N * M + 2 * N * M * M

F32 = mybir.dt.float32
BF16 = mybir.dt.bfloat16
I32 = mybir.dt.int32
U32 = mybir.dt.uint32
U8 = mybir.dt.uint8
FP8X4 = mybir.dt.float8_e4m3fn_x4
ACT = mybir.ActivationFunctionType
ALU = mybir.AluOpType

P = 128
HALF = 512
NT = N // P
B = (0, 1)
T_BANKS, RT_BANKS, U_BUFS, A_BUFS, R_BUFS, GROUP_BUFS = 3, 1, 3, 4, 4, 8

ORDER = [
    ('ly', 0, 0, 1),
    ('iy', 0, 0, 1, 'A'),
    ('ly', 1, 1),
    ('ly', 0, 0, 0),
    ('ly', 1, 0),
    ('ly', 0, 1),
    ('lx', 0, 0, 2),
    ('iy', 1, 1, 1, 'V'),
    ('lx', 1, 0, 2),
    ('iy', 1, 1, 0, 'A'),
    ('iy', 1, 0, 1, 'A'),
    ('lx', 1, 2, 4),
    ('iy', 0, 0, 0, 'V'),
    ('lx', 0, 2, 4),
    ('qy', 0, 0, (0, 1)),
    ('lk', 0, 1),
    ('iy', 1, 0, 0, 'V'),
    ('qy', 1, 1, (0, 1)),
    ('iy', 0, 1, 1, 'V'),
    ('iy', 0, 1, 0, 'A'),
    ('lk', 0, 2),
    ('qy', 1, 0, (0, 1)),
    ('ix', 0, 'A'),
    ('lk', 0, 3),
    ('qy', 0, 1, (0, 1)),
    ('lk', 0, 0),
    ('ix', 1, 'V'),
    ('qx', 0),
    ('lx', 1, 4, 8),
    ('s1', 0, 0),
    ('ix', 2, 'A'),
    ('lx', 0, 4, 8),
    ('qx', 1),
    ('s1', 0, 1),
    ('ix', 3, 'V'),
    ('D', 0, 0),
    ('s1', 1, 0),
    ('qx', 2),
    ('ik', 0, 3, 'V'),
    ('D', 0, 1),
    ('lw',),
    ('lk', 1, 3),
    ('C', 0, 0),
    ('ik', 0, 2, 'V'),
    ('ik', 0, 1, 'V'),
    ('qk', 0, (2, 3)),
    ('lk', 1, 1),
    ('ix', 4, 'V'),
    ('C', 0, 1),
    ('s1', 1, 1),
    ('qx', 3),
    ('E', 0, (0, 1)),
    ('D', 1, 0),
    ('w1',),
    ('s1', 2, 0),
    ('F', 0, (0, 1), 'V'),
    ('lk', 1, 0),
    ('D', 1, 1),
    ('C', 1, 0),
    ('ix', 5, 'V'),
    ('lk', 1, 2),
    ('C', 1, 1),
    ('qx', 4),
    ('s1', 2, 1),
    ('w2',),
    ('ik', 1, 3, 'V'),
    ('ik', 1, 0, 'V'),
    ('ix', 6, 'A'),
    ('E', 1, (0, 1)),
    ('D', 2, 0),
    ('s1', 3, 0),
    ('w3',),
    ('C', 2, 0),
    ('ik', 1, 2, 'V'),
    ('D', 2, 1),
    ('F', 1, (0, 1), 'V'),
    ('qx', 5),
    ('C', 2, 1),
    ('ta', 0, 0),
    ('ix', 7, 'V'),
    ('ta', 0, 1),
    ('s1', 3, 1),
    ('G', 0, 0),
    ('G', 0, 1),
    ('qx', 6),
    ('E', 2, (0, 1)),
    ('D', 3, 0),
    ('s1', 4, 0),
    ('ik', 0, 0, 'A'),
    ('C', 3, 0),
    ('D', 3, 1),
    ('ik', 1, 1, 'V'),
    ('F', 2, (0, 1), 'V'),
    ('ta', 1, 0),
    ('qk', 1, (0, 1)),
    ('ta', 1, 1),
    ('C', 3, 1),
    ('qx', 7),
    ('qa', 0, (0, 1)),
    ('G', 1, 0),
    ('s1', 4, 1),
    ('G', 1, 1),
    ('E', 3, (0, 1)),
    ('qk', 0, (0, 1)),
    ('D', 4, 0),
    ('C', 4, 0),
    ('ta', 2, 0),
    ('s1', 5, 0),
    ('D', 4, 1),
    ('ta', 2, 1),
    ('qk', 1, (2, 3)),
    ('qa', 1, (0, 1)),
    ('F', 3, (0, 1), 'V'),
    ('C', 4, 1),
    ('s2', 0, 0),
    ('G', 2, 0),
    ('G', 2, 1),
    ('s2', 0, 1),
    ('s1', 5, 1),
    ('ta', 3, 0),
    ('E', 4, (0, 1)),
    ('D', 5, 0),
    ('ta', 3, 1),
    ('C', 5, 0),
    ('H', 0, 0),
    ('H', 0, 1),
    ('so', 0, (0, 1)),
    ('D', 5, 1),
    ('s1', 6, 0),
    ('s2', 1, 0),
    ('qa', 2, (0, 1)),
    ('C', 5, 1),
    ('s2', 1, 1),
    ('G', 3, 0),
    ('F', 4, (0, 1), 'V'),
    ('G', 3, 1),
    ('ta', 4, 0),
    ('E', 5, (0, 1)),
    ('ta', 4, 1),
    ('I', 0, (0, 1), 'A'),
    ('H', 1, 0),
    ('H', 1, 1),
    ('D', 6, 0),
    ('s1', 6, 1),
    ('C', 6, 0),
    ('D', 6, 1),
    ('s2', 2, 0),
    ('s2', 2, 1),
    ('qa', 3, (0, 1)),
    ('s1', 7, 0),
    ('so', 1, (0, 1)),
    ('C', 6, 1),
    ('E', 6, (0, 1)),
    ('G', 4, 0),
    ('G', 4, 1),
    ('tr', 0, (0, 1)),
    ('H', 2, 0),
    ('H', 2, 1),
    ('I', 1, (0, 1), 'A'),
    ('F', 5, (0, 1), 'V'),
    ('D', 7, 0),
    ('s2', 3, 0),
    ('s1', 7, 1),
    ('V', 0, (0, 1), 'A'),
    ('C', 7, 0),
    ('D', 7, 1),
    ('s2', 3, 1),
    ('ta', 5, 0),
    ('ta', 5, 1),
    ('E', 7, (0,)),
    ('qa', 4, (0, 1)),
    ('C', 7, 1),
    ('H', 3, 0),
    ('H', 3, 1),
    ('I', 2, (0, 1), 'A'),
    ('s2', 4, 0),
    ('tr', 1, (0, 1)),
    ('G', 5, 0),
    ('so', 2, (0, 1)),
    ('G', 5, 1),
    ('s2', 4, 1),
    ('F', 6, (0, 1), 'V'),
    ('V', 1, (0, 1), 'A'),
    ('qr', 0, (0, 1)),
    ('H', 4, 0),
    ('H', 4, 1),
    ('I', 3, (0, 1), 'A'),
    ('ta', 6, 0),
    ('qa', 5, (0, 1)),
    ('ta', 6, 1),
    ('tr', 2, (0, 1)),
    ('E', 7, (1,)),
    ('G', 6, 0),
    ('G', 6, 1),
    ('so', 3, (0, 1)),
    ('F', 7, (0,), 'V'),
    ('V', 2, (0, 1), 'A'),
    ('I', 4, (0, 1), 'A'),
    ('s2', 5, 0),
    ('qr', 1, (0, 1)),
    ('s2', 5, 1),
    ('F', 7, (1,), 'V'),
    ('tr', 3, (0, 1)),
    ('qa', 6, (0, 1)),
    ('H', 5, 0),
    ('H', 5, 1),
    ('ta', 7, 0),
    ('ta', 7, 1),
    ('V', 3, (0, 1), 'A'),
    ('G', 7, 0),
    ('G', 7, 1),
    ('so', 4, (0, 1)),
    ('qr', 2, (0, 1)),
    ('tr', 4, (0, 1)),
    ('s2', 6, 0),
    ('I', 5, (0, 1), 'A'),
    ('s2', 6, 1),
    ('qa', 7, (0,)),
    ('V', 4, (0, 1), 'A'),
    ('qa', 7, (1,)),
    ('H', 6, 0),
    ('H', 6, 1),
    ('qr', 3, (0, 1)),
    ('sw', 0, 1),
    ('tr', 5, (0, 1)),
    ('s2', 7, 0),
    ('s2', 7, 1),
    ('I', 6, (0, 1), 'A'),
    ('qr', 4, (0, 1)),
    ('so', 5, (0, 1)),
    ('V', 5, (0, 1), 'V'),
    ('H', 7, 0),
    ('H', 7, 1),
    ('tr', 6, (0, 1)),
    ('sw', 1, 2),
    ('I', 7, (0,), 'V'),
    ('I', 7, (1,), 'V'),
    ('V', 6, (0, 1), 'A'),
    ('tr', 7, (0,)),
    ('qr', 5, (0, 1)),
    ('so', 6, (0, 1)),
    ('sw', 2, 3),
    ('tr', 7, (1,)),
    ('V', 7, (0,), 'A'),
    ('sw', 3, 4),
    ('qr', 6, (0, 1)),
    ('V', 7, (1,), 'A'),
    ('so', 7, (0,)),
    ('sw', 4, 5),
    ('qr', 7, (0,)),
    ('qr', 7, (1,)),
    ('so', 7, (1,)),
    ('sw', 5, 6),
    ('sw', 6, 7),
    ('sw', 7, 8),
    ('ss', 0),
    ('ss', 1),
    ('ss', 2),
    ('ss', 3),
]


def tile_signedcrossclimatenetworktriangles_x1_kernel(tc, x, y, w, k, out_0, out_1, out_2):
    nc = tc.nc
    with ExitStack() as ctx:
        keep = ctx.enter_context(tc.tile_pool(name="keep", bufs=1))
        psum = ctx.enter_context(tc.psum_pool(name="psum", bufs=1))
        ctx.enter_context(tc.manual_schedule())

        ident = keep.tile([P, P], F32, name="ident")
        minus4 = keep.tile([P, 1], F32, name="minus4")
        warm = keep.tile([P, 1], F32, name="warm")
        w_rows = keep.tile([P, P], BF16, name="w_rows")
        w_rows32 = keep.tile([P, P], F32, name="w_rows32")
        w_cols = keep.tile([P, 8], F32, name="w_cols")
        x_codes = keep.tile([P, NT, 2, P], U32, name="x_codes", align_bytes=64)
        x_scales = keep.tile([P, NT, 2, P], U8, name="x_scales", align_bytes=64)
        y_codes = keep.tile([P, 2, M], U32, name="y_codes", align_bytes=64)
        y_scales = keep.tile([P, 2, M], U8, name="y_scales", align_bytes=64)
        k_codes = keep.tile([P, 2, M], U32, name="k_codes", align_bytes=64)
        k_scales = keep.tile([P, 2, M], U8, name="k_scales", align_bytes=64)
        r_codes = keep.tile([P, 2, N], U32, name="r_codes", align_bytes=64)
        r_scales = keep.tile([P, 2, N], U8, name="r_scales", align_bytes=64)
        tiles = {}

        def sb(kind, index, shape, dtype, depth):
            key = (kind, index)
            if key not in tiles:
                tiles[key] = keep.tile(shape, dtype, name="%s%d" % (kind, index % depth), align_bytes=64)
            return tiles[key]

        def bank(kind, index, depth):
            key = (kind, index)
            if key not in tiles:
                tiles[key] = psum.tile([P, HALF], F32, name="%s%d" % (kind, index % depth))
            return tiles[key]

        def copy(eng, out, in_):
            if eng == "V":
                nc.vector.tensor_copy(out=out, in_=in_)
            elif eng == "A":
                nc.scalar.copy(out=out, in_=in_)
            else:
                nc.gpsimd.tensor_scalar(out=out, in0=in_, scalar1=1.0, scalar2=1.0, op0=ALU.mult, op1=ALU.mult)

        def quantize(codes, scales, in_):
            nc.vector.quantize_mx(out=codes.bitcast(FP8X4), scales=scales, in_=in_)

        def mx_product(acc, lhs_codes, lhs_scales, rhs_codes, rhs_scales, cols):
            for c in B:
                nc.tensor.matmul_mx(
                    out=acc[:],
                    lhsT=lhs_codes[:, c, :].bitcast(FP8X4),
                    lhsT_scale=lhs_scales[:, c, :],
                    rhs=rhs_codes[:, c, cols].bitcast(FP8X4),
                    rhs_scale=rhs_scales[:, c, cols],
                    start=(c == 0),
                    stop=(c == 1),
                )

        def half(g):
            return slice(g * HALF, (g + 1) * HALF)

        def span(gs, width):
            return slice(gs[0] * width, (gs[-1] + 1) * width)

        y_raw = {}
        x_raw = {}
        k_raw = {}

        def ly(c, h, q=None):
            first, width = (h * HALF, HALF) if q is None else (h * HALF + q * 256, 256)
            raw = keep.tile([P, 4, width], BF16, name="y_raw%d_%d" % (c, first))
            nc.sync.dma_start(
                out=raw[:], in_=y[half(c), first : first + width].rearrange("(p j) m -> p j m", j=4)
            )
            for piece in range(width // 256):
                y_raw[(c, first // 256 + piece)] = raw[:, :, piece * 256 : (piece + 1) * 256]

        def lx(c, i0, i1):
            if (i0, i1) not in x_raw:
                x_raw[(i0, i1)] = keep.tile([P, 2, 4, (i1 - i0) * P], BF16, name="x_raw%d" % i0)
            nc.sync.dma_start(
                out=x_raw[(i0, i1)][:, c],
                in_=x[half(c), i0 * P : i1 * P].rearrange("(p j) n -> p j n", j=4),
            )

        def lk(g, j):
            if g not in k_raw:
                k_raw[g] = keep.tile([P, 4, M], BF16, name="k_raw%d" % g)
            nc.sync.dma_start(
                out=k_raw[g][:, j, :],
                in_=k[half(g), :].rearrange("(b j r) q -> j b r q", j=4, r=8)[j],
            )

        def lw():
            for g in B:
                nc.sync.dma_start(
                    out=w_rows[4 * g : 4 * g + 4, :].rearrange("t (b r) -> t b r", r=8),
                    in_=w[half(g)].rearrange("(b t r) -> t b r", t=4, r=8),
                )

        def w1():
            nc.scalar.copy(out=w_rows32[0:8, :], in_=w_rows[0:8, :])

        def w2():
            nc.tensor.transpose(bank("rt", -1, RT_BANKS)[:, 0:P], w_rows32[:], ident[:])

        def w3():
            nc.scalar.copy(out=w_cols[:], in_=tiles[("rt", -1)][:, 0:8])

        def interleave(eng, dst, src):
            copy(eng, dst.rearrange("p (c i t) -> p c t i", i=4, t=4), src.rearrange("p t (c i) -> p c t i", i=4))

        def iy(c, h, q, eng):
            g = sb("yk_grouped", 2 * h + c, [P, 2048], BF16, GROUP_BUFS)
            interleave(eng, g[:, q * 1024 : (q + 1) * 1024], y_raw[(c, 2 * h + q)])

        def qy(c, h, qs):
            g = tiles[("yk_grouped", 2 * h + c)]
            cols = slice(h * HALF + qs[0] * 256, h * HALF + (qs[-1] + 1) * 256)
            quantize(y_codes[:, c, cols], y_scales[:, c, cols], g[:, span(qs, 1024)])

        def ik(g, q, eng):
            grouped = sb("yk_grouped", 4 + 2 * (q // 2) + g, [P, 2048], BF16, GROUP_BUFS)
            interleave(eng, grouped[:, (q % 2) * 1024 : (q % 2 + 1) * 1024], k_raw[g][:, :, q * 256 : (q + 1) * 256])

        def qk(g, qs):
            grouped = tiles[("yk_grouped", 4 + 2 * (qs[0] // 2) + g)]
            cols = span(qs, 256)
            quantize(k_codes[:, g, cols], k_scales[:, g, cols], grouped[:, span([q % 2 for q in qs], 1024)])

        def ix(i, eng):
            i0, i1 = [key for key in x_raw if key[0] <= i < key[1]][0]
            src = x_raw[(i0, i1)][:, :, :, (i - i0) * P : (i - i0 + 1) * P]
            grouped = sb("x_grouped", i, [P, 1024], BF16, 3)
            if eng == "G":
                for c in B:
                    interleave(eng, grouped[:, half(c)], src[:, c])
            else:
                copy(
                    eng,
                    grouped[:].rearrange("p (c n i t) -> p c n t i", c=2, i=4, t=4),
                    src.rearrange("p c t (n i) -> p c n t i", i=4),
                )

        def qx(i):
            quantize(
                x_codes[:, i].rearrange("p c n -> p (c n)"),
                x_scales[:, i].rearrange("p c n -> p (c n)"),
                tiles[("x_grouped", i)][:],
            )

        def s1(i, g):
            mx_product(bank("t", 2 * i + g, T_BANKS), x_codes[:, i], x_scales[:, i], y_codes, y_scales, half(g))

        def from_t(i, g, kind, func, scale):
            dst = sb(kind, i, [P, M], F32, U_BUFS)
            nc.scalar.activation(
                out=dst[:, half(g)].rearrange("n (t b r) -> n t b r", t=4, r=8),
                in_=tiles[("t", 2 * i + g)][:].rearrange("n (b t r) -> n t b r", t=4, r=8),
                func=func,
                scale=scale,
            )

        def op_c(i, g):
            from_t(i, g, "tanh", ACT.Tanh, 1.0 / 32.0)

        def op_d(i, g):
            from_t(i, g, "mag", ACT.Abs, 1.0)

        def op_e(i, gs):
            gate = sb("gate", i, [P, M], F32, U_BUFS)
            cols = span(gs, HALF)
            nc.scalar.activation(
                out=gate[:, cols], in_=tiles[("mag", i)][:, cols], func=ACT.Sigmoid, scale=4.0 / 32.0, bias=minus4[:]
            )

        def op_f(i, gs, eng):
            link = sb("link", i, [P, M], F32, A_BUFS)
            cols = span(gs, HALF)
            engine = nc.vector if eng == "V" else nc.gpsimd
            engine.tensor_tensor(
                out=link[:, cols], in0=tiles[("tanh", i)][:, cols], in1=tiles[("gate", i)][:, cols], op=ALU.mult
            )

        def ta(i, g):
            turned = bank("at", 2 * i + g, 2)
            for t in range(4):
                first = g * HALF + t * P
                nc.tensor.transpose(turned[:, t * P : (t + 1) * P], tiles[("link", i)][:, first : first + P], ident[:])

        def op_g(i, g):
            grouped = sb("aw_grouped", i, [P, M], BF16, 2)
            nc.vector.tensor_tensor(
                out=grouped[:, half(g)].rearrange("p (n t) -> p n t", t=4),
                in0=tiles[("at", 2 * i + g)][:].rearrange("p (t n) -> p n t", t=4),
                in1=w_cols[:, 4 * g : 4 * g + 4].unsqueeze(1).to_broadcast([P, P, 4]),
                op=ALU.mult,
            )

        def qa(i, gs):
            codes = sb("aw_codes", i, [P, 2 * P], U32, 2)
            scales = sb("aw_scales", i, [P, 2 * P], U8, 2)
            quantize(codes[:, span(gs, P)], scales[:, span(gs, P)], tiles[("aw_grouped", i)][:, span(gs, HALF)])

        def s2(i, h):
            mx_product(
                bank("path", 2 * i + h, 2),
                tiles[("aw_codes", i)][:].rearrange("p (g n) -> p g n", g=2),
                tiles[("aw_scales", i)][:].rearrange("p (g n) -> p g n", g=2),
                k_codes,
                k_scales,
                half(h),
            )

        def op_h(i, h):
            result = sb("result", i, [P, M], F32, R_BUFS)
            nc.vector.tensor_tensor(
                out=result[:, half(h)].rearrange("n (b t r) -> n b t r", t=4, r=8),
                in0=tiles[("path", 2 * i + h)][:].rearrange("n (b t r) -> n b t r", t=4, r=8),
                in1=tiles[("link", i)][:, half(h)].rearrange("n (t b r) -> n b t r", t=4, r=8),
                op=ALU.mult,
            )

        def op_i(i, gs, eng):
            pairs = sb("pairs", i, [P, 2, 2 * P, 2], BF16, 2)
            copy(
                eng,
                pairs[:, :, span(gs, P), :],
                tiles[("result", i)][:, span(gs, HALF)].rearrange("n (p u e) -> n u p e", u=2, e=2),
            )

        def tr(i, gs):
            turned = bank("rt", i, RT_BANKS)
            words = tiles[("pairs", i)][:].rearrange("n u p e -> n (u p e)").bitcast(F32)
            for g in gs:
                for u in B:
                    first = u * 2 * P + g * P
                    nc.tensor.transpose(
                        turned[:, (2 * g + u) * P : (2 * g + u + 1) * P], words[:, first : first + P], ident[:]
                    )

        def op_v(i, gs, eng):
            grouped = sb("r_grouped", i, [P, M], BF16, 2)
            cols = span(gs, 2 * P)
            copy(
                eng,
                grouped[:].bitcast(F32)[:, cols].rearrange("p (g n u) -> p g n u", n=P, u=2),
                tiles[("rt", i)][:, cols].rearrange("p (g u n) -> p g n u", n=P, u=2),
            )

        def qr(i, gs):
            for g in gs:
                cols = slice(i * P, (i + 1) * P)
                quantize(r_codes[:, g, cols], r_scales[:, g, cols], tiles[("r_grouped", i)][:, half(g)])

        def so(i, gs):
            cols = span(gs, HALF)
            nc.sync.dma_start(out=out_0[i * P : (i + 1) * P, cols], in_=tiles[("result", i)][:, cols])

        def sw(i0, i1):
            cols = slice(i0 * P, i1 * P)
            nc.sync.dma_start(
                out=out_1.rearrange("g p n t -> p g (n t)").bitcast(I32)[:, :, cols],
                in_=r_codes[:].bitcast(I32)[:, :, cols],
            )

        def ss(quad):
            nc.sync.dma_start(
                out=out_2[:, 4 * quad : 4 * quad + 4, :].rearrange("g r n -> r g n").bitcast(I32),
                in_=r_scales[32 * quad : 32 * quad + 4].bitcast(I32),
            )

        nc.gpsimd.memset(minus4[:], -4.0)
        nc.scalar.activation(out=warm[:], in_=minus4[:], func=ACT.Sigmoid)
        nc.gpsimd.memset(w_rows32[:], 0.0)
        make_identity(nc, ident[:])

        steps = {
            "ly": ly, "lx": lx, "lk": lk, "lw": lw, "w1": w1, "w2": w2, "w3": w3, "iy": iy, "qy": qy, "ik": ik, "qk": qk, "ix": ix, "qx": qx,
            "s1": s1, "C": op_c, "D": op_d, "E": op_e, "F": op_f, "ta": ta, "G": op_g, "qa": qa, "s2": s2,
            "H": op_h, "I": op_i, "tr": tr, "V": op_v, "qr": qr, "so": so, "sw": sw, "ss": ss,
        }
        for step in ORDER:
            steps[step[0]](*step[1:])
